import numpy as np
import ml_dtypes


def mxq(x, axis, fmt="e4m3"):
    dtype, down = {"e4m3": (ml_dtypes.float8_e4m3fn, 7), "e5m2": (ml_dtypes.float8_e5m2, 14)}[fmt]
    v = np.moveaxis(np.asarray(x, np.float32).astype(ml_dtypes.bfloat16).astype(np.float64), axis, -1)
    blocks = v.reshape(v.shape[:-1] + (-1, 32))
    amax = np.abs(blocks).max(-1, keepdims=True)
    byte = np.maximum(np.where(amax > 0, np.frexp(amax)[1] - 1 + 127, 0) - down, 1)
    scale = np.exp2(byte - 127.0)
    codes = (blocks / scale).astype(np.float32).astype(dtype).astype(np.float64)
    return np.moveaxis((codes * scale).reshape(v.shape), -1, axis)


WIDE = False


def mx_kscale(k):
    if not WIDE:
        return np.ones(k)
    levels = np.array([30, -30])
    if k % 512:
        return np.exp2(np.random.permutation(np.resize(levels, k // 32))).repeat(32)
    a = np.empty((k // 512, 16))
    for p in range(k // 512):
        a[p, :8] = np.random.permutation(np.resize(levels, 8))
        for g in range(8):
            far = levels[np.abs(levels - a[p, g]) >= 10]
            a[p, g + 8] = far[np.random.randint(len(far))]
    return np.exp2(a.ravel()).repeat(32)


def f64(x):
    return np.asarray(x).astype(np.float64)


def striped(idx):
    return np.tile(np.asarray(idx).reshape(-1, 16).T, (8, 1)).astype(np.uint16)


def unstriped(offs):
    return offs[:16].T.reshape(-1).astype(np.int64)


E2M1 = np.array([0.0, 0.5, 1.0, 1.5, 2.0, 3.0, 4.0, 6.0, -0.0, -0.5, -1.0, -1.5, -2.0, -3.0, -4.0, -6.0])


def pack_weight(w, fmt):
    k, n = w.shape
    w = f64(np.asarray(w, np.float32).astype(ml_dtypes.bfloat16)).reshape(k // 32, 32, n)
    amax = np.abs(w).max(1)
    if fmt in ("e4m3", "e5m2"):
        byte = np.frexp(amax)[1] - 1 + 127 - (7 if fmt == "e4m3" else 14)
    else:
        mant, ex = np.frexp(amax / 6.0)
        byte = np.where(mant > 0.5, ex, ex - 1) + 127
    byte = np.clip(np.where(amax > 0, byte, 1), 1, 254)
    scaled = (w * np.exp2(127.0 - byte)[:, None, :]).reshape(k, n).astype(np.float32)
    by_word = np.ascontiguousarray(scaled.reshape(k // 512, 128, 4, n).transpose(0, 1, 3, 2))
    if fmt in ("e4m3", "e5m2"):
        words = by_word.astype(ml_dtypes.float8_e4m3fn if fmt == "e4m3" else ml_dtypes.float8_e5m2).view(np.uint8)
    else:
        c = by_word.astype(ml_dtypes.float4_e2m1fn).view(np.uint8) & 0xF
        words = (c[..., 0::2] | (c[..., 1::2] << 4)).reshape(k // 512, 128, 2 * n)
    return np.ascontiguousarray(words), np.ascontiguousarray(byte.astype(np.uint8).reshape(k // 512, 16, n))


def unpack_weight(words, scales, fmt):
    g, _, n = scales.shape
    words = np.ascontiguousarray(words).reshape(g, 128, n, -1)
    if fmt in ("e4m3", "e5m2"):
        vals = words.view(ml_dtypes.float8_e4m3fn if fmt == "e4m3" else ml_dtypes.float8_e5m2).astype(np.float64)
    else:
        nib = np.empty((g, 128, n, 4), np.uint8)
        nib[..., 0::2] = words & 0xF
        nib[..., 1::2] = words >> 4
        vals = E2M1[nib]
    vals = vals * np.repeat(np.exp2(scales.astype(np.float64) - 127.0), 8, axis=1)[..., None]
    return vals.transpose(0, 1, 3, 2).reshape(g * 512, n)


K, T, J, R, C, O, N = 512, 2048, 256, 512, 512, 128, 256


def setup_inputs():
    n = np.random.standard_normal
    idx = np.random.permutation(T)[:J]
    idx2 = np.random.permutation(T)[:J]
    idx3 = np.random.permutation(C)[:J]
    idx4 = np.random.permutation(C)[:J]
    idx5 = np.random.permutation(J)[:J]
    idx6 = np.random.permutation(J)[:O]
    idx7 = np.random.permutation(J)[:O]
    fk = mx_kscale(K)
    fr = mx_kscale(R)
    xtp = pack_weight(n((K, T)) / fk[:, None], "e2m1")
    wp = pack_weight(n((K, R)) * 1 / np.sqrt(K) * fk[:, None] * fr, "e5m2")
    w2p = pack_weight(n((K, R)) * 1 / np.sqrt(K) * fk[:, None], "e4m3")
    wbp = pack_weight(n((R, N)) * 1 / np.sqrt(R) / fr[:, None], "e4m3")
    return {
        "xt_words": xtp[0],
        "xt_scales": xtp[1],
        "w_words": wp[0],
        "w_scales": wp[1],
        "w2_words": w2p[0],
        "w2_scales": w2p[1],
        "wb_words": wbp[0],
        "wb_scales": wbp[1],
        "offs": striped(idx),
        "offs2": striped(idx2),
        "offs3": striped(idx3),
        "offs4": striped(idx4),
        "offs5": striped(idx5),
        "offs6": striped(idx6),
        "offs7": striped(idx7),
    }


def reference(xt_words, xt_scales, w_words, w_scales, w2_words, w2_scales, wb_words, wb_scales, offs, offs2, offs3, offs4, offs5, offs6, offs7):
    idx = unstriped(offs)
    idx2 = unstriped(offs2)
    idx3 = unstriped(offs3)
    idx4 = unstriped(offs4)
    idx5 = unstriped(offs5)
    idx6 = unstriped(offs6)
    idx7 = unstriped(offs7)
    xtu = unpack_weight(xt_words, xt_scales, "e2m1")
    wu = unpack_weight(w_words, w_scales, "e5m2")
    w2u = unpack_weight(w2_words, w2_scales, "e4m3")
    wbu = unpack_weight(wb_words, wb_scales, "e4m3")
    xtidxg = xtu[:, idx]
    a = wu.T @ xtidxg
    xtidx2g = xtu[:, idx2]
    b = w2u.T @ xtidx2g
    lb = b[:, 0:1]
    la = a[:, 0:1]
    lb2 = b[:, 128:129]
    pw = np.zeros((R, C))
    pw[:, idx3] = a
    rb = np.maximum(pw[:, idx4] * lb, b[:, idx5] * la)
    hid = np.abs(rb[:, idx6] - rb[:, idx7] * lb2)
    hidq = mxq(hid, 0, "e5m2")
    y = wbu.T @ hidq
    return y

from contextlib import ExitStack

import concourse.mybir as mybir

K, T, J, R, C, O, N = 512, 2048, 256, 512, 512, 128, 256
FLOPS = 2 * (2 * K * R * J) + 2 * R * N * O

F32 = mybir.dt.float32
BF16 = mybir.dt.bfloat16
I32 = mybir.dt.int32
U32 = mybir.dt.uint32
U16 = mybir.dt.uint16
U8 = mybir.dt.uint8
E4M3 = mybir.dt.float8_e4m3fn_x4
E5M2 = mybir.dt.float8_e5m2_x4
E2M1 = mybir.dt.float4_e2m1fn_x4
ACT = mybir.ActivationFunctionType
ALU = mybir.AluOpType

P = 128
PACK = 4
QUADS = 4


def tile_list_leadanswer_ahead_one_plain_kernel(
    tc, xt_words, xt_scales, w_words, w_scales, w2_words, w2_scales, wb_words, wb_scales,
    offs, offs2, offs3, offs4, offs5, offs6, offs7, out,
):
    nc = tc.nc
    with ExitStack() as ctx:
        sb = ctx.enter_context(tc.tile_pool(name="sb", bufs=1))
        ps = ctx.enter_context(tc.psum_pool(name="ps", bufs=1))

        def tile(shape, dtype, name):
            return sb.tile(shape, dtype, name=name, align_bytes=64)

        def load_list(src, name):
            dst = tile(list(src.shape), U16, name)
            nc.sync.dma_start(dst[:], src)
            return dst

        def load_words(src, cols, name):
            dst = tile([P, cols], U32, name)
            nc.sync.dma_start(out=dst[:].bitcast(I32), in_=src[0].rearrange("p n t -> p (n t)").bitcast(I32))
            return dst

        def load_scale_rows(queue, plane, src):
            for q in range(QUADS):
                queue.dma_start(out=plane[32 * q : 32 * q + 4, :].bitcast(I32), in_=src[0, 4 * q : 4 * q + 4, :].bitcast(I32))

        def load_staged_scales(src, name):
            dst = tile([4, QUADS, R // 4], I32, name)
            nc.sync.dma_start(out=dst[:], in_=src[0].bitcast(I32).rearrange("(q r) c -> r q c", r=4))
            return dst

        def zeroed(shape, dtype, name):
            dst = tile(shape, dtype, name)
            nc.vector.memset(dst[:].bitcast(I32), 0)
            return dst

        def deal_scales(spread, name):
            dealt = tile([P, R], U8, name)
            nc.vector.tensor_copy(out=dealt[:].rearrange("p (t m) -> p m t", t=PACK), in_=spread[:].rearrange("p (m t) -> p m t", t=PACK))
            return dealt

        def deal_words(copy, raw, name):
            dealt = tile([P, R], U32, name)
            copy(out=dealt[:].rearrange("p (t m) -> p m t", t=PACK), in_=raw[:].rearrange("p (m t) -> p m t", t=PACK))
            return dealt

        x_plane = zeroed([P, T], U8, "x_plane")
        w_spread = zeroed([P, R], U8, "w_spread")
        w2_spread = zeroed([P, R], U8, "w2_spread")

        w_staged = load_staged_scales(w_scales, "w_staged")
        l1 = load_list(offs, "l1")
        x_words = tile([P, T], U16, "x_words")
        nc.sync.dma_start(out=x_words[:].bitcast(I32), in_=xt_words[0].bitcast(I32))
        load_scale_rows(nc.sync, x_plane, xt_scales)
        w_raw = load_words(w_words, R, "w_raw")
        l2 = load_list(offs2, "l2")
        load_scale_rows(nc.sync, w2_spread, w2_scales)
        w2_raw = load_words(w2_words, R, "w2_raw")
        l3 = load_list(offs3, "l3")
        l4 = load_list(offs4, "l4")
        l5 = load_list(offs5, "l5")
        l7 = load_list(offs7, "l7")
        l6 = load_list(offs6, "l6")
        wb_codes = load_words(wb_words, N, "wb_codes")

        boards = []
        for t in range(PACK):
            board = tile([P, C], F32, f"board{t}")
            nc.vector.memset(board[:], 0.0)
            boards.append(board)
        wb_plane = zeroed([P, N], U8, "wb_plane")
        load_scale_rows(nc.sync, wb_plane, wb_scales)

        def pick(lst, name):
            words = tile([P, J], U16, name + "_words")
            nc.vector.tensor_copy(out=words[:], in_=x_words[:].indirect(lst[:]))
            scales = tile([P, J], U8, name + "_scales")
            nc.vector.tensor_copy(out=scales[:], in_=x_plane[:].indirect(lst[:]))
            return words, scales

        def first_stage(codes, plane, fmt, picked, name):
            banks = []
            for t in range(PACK):
                bank = ps.tile([P, J], F32, name=f"{name}{t}")
                cols = slice(t * P, (t + 1) * P)
                nc.tensor.matmul_mx(out=bank[:], lhsT=codes[:, cols].bitcast(fmt), lhsT_scale=plane[:, cols],
                                    rhs=picked[0][:].bitcast(E2M1), rhs_scale=picked[1][:], start=True, stop=True)
                banks.append(bank)
            return banks

        for q in range(QUADS):
            nc.vector.tensor_copy(out=w_spread[32 * q : 32 * q + 4, :].bitcast(I32), in_=w_staged[:, q, :])
        w_plane = deal_scales(w_spread, "w_plane")
        picked1 = pick(l1, "x1")
        w_codes = deal_words(nc.vector.tensor_copy, w_raw, "w_codes")
        a_banks = first_stage(w_codes, w_plane, E5M2, picked1, "a_bank")
        picked2 = pick(l2, "x2")
        w2_plane = deal_scales(w2_spread, "w2_plane")

        a = [tile([P, J], F32, f"a{t}") for t in range(PACK)]
        b = [tile([P, 2 * J], F32, f"b{t}") for t in range(PACK)]
        left = [tile([P, J], F32, f"left{t}") for t in range(PACK)]
        right = [tile([P, J], F32, f"right{t}") for t in range(PACK)]
        rb = [tile([P, J], F32, f"rb{t}") for t in range(PACK)]
        far = [tile([P, O], F32, f"far{t}") for t in range(PACK)]
        diff = tile([P, PACK, O], F32, "diff")

        def copy_out(on_scalar, dst, bank):
            if on_scalar:
                nc.scalar.activation(out=dst, in_=bank[:], func=ACT.Copy)
            else:
                nc.vector.tensor_copy(out=dst, in_=bank[:])

        def put(t, on_scalar):
            if on_scalar:
                nc.scalar.activation(out=boards[t][:].indirect(l3[:]), in_=a[t][:], func=ACT.Copy)
            else:
                nc.vector.tensor_copy(out=boards[t][:].indirect(l3[:]), in_=a[t][:])

        def look_left(t):
            nc.scalar.activation(out=left[t][:], in_=boards[t][:].indirect(l4[:]), func=ACT.Copy, scale=b[t][:, 0:1])

        def look_right(t):
            nc.scalar.activation(out=right[t][:], in_=b[t][:].indirect(l5[:]), func=ACT.Copy, scale=a[t][:, 0:1])

        def larger(t):
            nc.vector.tensor_tensor(out=rb[t][:], in0=left[t][:], in1=right[t][:], op=ALU.max)

        def look_far(t):
            nc.scalar.activation(out=far[t][:], in_=rb[t][:].indirect(l7[:]), func=ACT.Copy, scale=b[t][:, 128:129])

        def differ(t):
            nc.vector.tensor_tensor(out=diff[:, t, :], in0=rb[t][:].indirect(l6[:]), in1=far[t][:], op=ALU.subtract)

        copy_out(True, a[0][:], a_banks[0])
        w2_codes = deal_words(nc.scalar.copy, w2_raw, "w2_codes")
        b_banks = first_stage(w2_codes, w2_plane, E4M3, picked2, "b_bank")
        put(0, True)
        copy_out(False, a[1][:], a_banks[1])
        put(1, False)
        copy_out(True, b[0][:, 0:J], b_banks[0])
        look_left(0)
        look_right(0)
        copy_out(False, a[2][:], a_banks[2])
        put(2, False)
        copy_out(True, b[1][:, 0:J], b_banks[1])
        look_left(1)
        look_right(1)
        copy_out(False, b[2][:, 0:J], b_banks[2])
        larger(0)
        look_far(0)
        copy_out(False, a[3][:], a_banks[3])
        put(3, False)
        look_left(2)
        look_right(2)
        copy_out(True, b[3][:, 0:J], b_banks[3])
        look_right(3)
        larger(1)
        look_far(1)
        differ(0)
        larger(2)
        look_left(3)
        look_far(2)
        differ(1)
        larger(3)
        look_far(3)
        differ(2)
        differ(3)

        hid = tile([P, O, PACK], BF16, "hid")
        turned = diff[:].rearrange("p t o -> p o t")
        half = O // 2
        nc.vector.scalar_tensor_tensor(out=hid[:, 0:half, :], in0=turned[:, 0:half, :], scalar=-1.0, in1=turned[:, 0:half, :],
                                       op0=ALU.mult, op1=ALU.max)
        nc.scalar.activation(out=hid[:, half:O, :], in_=turned[:, half:O, :], func=ACT.Abs)
        hid_codes = tile([P, O], U32, "hid_codes")
        hid_plane = tile([P, O], U8, "hid_plane")
        nc.vector.quantize_mx(out=hid_codes[:].bitcast(E5M2), scales=hid_plane[:], in_=hid[:].rearrange("p o t -> p (o t)"))

        for h in range(N // P):
            cols = slice(h * P, (h + 1) * P)
            bank = ps.tile([P, O], F32, name=f"a_bank{h}")
            nc.tensor.matmul_mx(out=bank[:], lhsT=wb_codes[:, cols].bitcast(E4M3), lhsT_scale=wb_plane[:, cols],
                                rhs=hid_codes[:].bitcast(E5M2), rhs_scale=hid_plane[:], start=True, stop=True)
            y = tile([P, O], F32, f"y{h}")
            copy_out(h == 1, y[:], bank)
            (nc.scalar if h == 1 else nc.sync).dma_start(out=out[cols, :], in_=y[:])
